import numpy as np
import ml_dtypes


def mxq(x, axis, fmt="e4m3"):
    dtype, down = {"e4m3": (ml_dtypes.float8_e4m3fn, 7), "e5m2": (ml_dtypes.float8_e5m2, 14)}[fmt]
    v = np.moveaxis(np.asarray(x, np.float32).astype(ml_dtypes.bfloat16).astype(np.float64), axis, -1)
    blocks = v.reshape(v.shape[:-1] + (-1, 32))
    amax = np.abs(blocks).max(-1, keepdims=True)
    byte = np.maximum(np.where(amax > 0, np.frexp(amax)[1] - 1 + 127, 0) - down, 1)
    scale = np.exp2(byte - 127.0)
    codes = (blocks / scale).astype(np.float32).astype(dtype).astype(np.float64)
    return np.moveaxis((codes * scale).reshape(v.shape), -1, axis)


WIDE = False


def mx_kscale(k):
    if not WIDE:
        return np.ones(k)
    levels = np.array([10, -10, 5, -5, 0])
    if k % 512:
        return np.exp2(np.random.permutation(np.resize(levels, k // 32))).repeat(32)
    a = np.empty((k // 512, 16))
    for p in range(k // 512):
        a[p, :8] = np.random.permutation(np.resize(levels, 8))
        for g in range(8):
            far = levels[np.abs(levels - a[p, g]) >= 10]
            a[p, g + 8] = far[np.random.randint(len(far))]
    return np.exp2(a.ravel()).repeat(32)


BF16 = ml_dtypes.bfloat16


def bf(x):
    return np.asarray(x, np.float32).astype(BF16)


def f64(x):
    return np.asarray(x).astype(np.float64)


E2M1 = np.array([0.0, 0.5, 1.0, 1.5, 2.0, 3.0, 4.0, 6.0, -0.0, -0.5, -1.0, -1.5, -2.0, -3.0, -4.0, -6.0])


def pack_weight(w, fmt):
    k, n = w.shape
    w = f64(bf(w)).reshape(k // 32, 32, n)
    amax = np.abs(w).max(1)
    if fmt == "e4m3":
        byte = np.frexp(amax)[1] - 1 + 127 - 7
    else:
        mant, ex = np.frexp(amax / 6.0)
        byte = np.where(mant > 0.5, ex, ex - 1) + 127
    byte = np.clip(np.where(amax > 0, byte, 1), 1, 254)
    scaled = (w * np.exp2(127.0 - byte)[:, None, :]).reshape(k, n).astype(np.float32)
    by_word = np.ascontiguousarray(scaled.reshape(k // 512, 128, 4, n).transpose(0, 1, 3, 2))
    if fmt == "e4m3":
        words = by_word.astype(ml_dtypes.float8_e4m3fn).view(np.uint8)
    else:
        c = by_word.astype(ml_dtypes.float4_e2m1fn).view(np.uint8) & 0xF
        words = c[..., 0::2] | (c[..., 1::2] << 4)
    return np.ascontiguousarray(words), np.ascontiguousarray(byte.astype(np.uint8).reshape(k // 512, 16, n))


def unpack_weight(words, scales, fmt):
    g, p, n, _ = words.shape
    if fmt == "e4m3":
        vals = np.ascontiguousarray(words).view(ml_dtypes.float8_e4m3fn).astype(np.float64)
    else:
        nib = np.empty((g, p, n, 4), np.uint8)
        nib[..., 0::2] = words & 0xF
        nib[..., 1::2] = words >> 4
        vals = E2M1[nib]
    vals = vals * np.repeat(np.exp2(scales.astype(np.float64) - 127.0), 8, axis=1)[..., None]
    return vals.transpose(0, 1, 3, 2).reshape(g * 512, n)


B, I, J, Z, H, O = 1024, 64, 32, 1024, 1024, 512
Q = I * J


def row_outer(u, v):
    outer = u[:, :, None] * v[:, None, :]
    return outer.reshape(u.shape[0], u.shape[1] * v.shape[1])


def leaky(s):
    return np.maximum(s, 0.0) + 0.25 * np.minimum(s, 0.0)


def draw0():
    sz, t = mx_kscale(Z), mx_kscale(H)
    su = mx_kscale(Q)[::J]
    z = bf(np.random.standard_normal((B, Z)) * sz)
    u = bf(np.random.standard_normal((B, I)) * su)
    v = bf(np.random.standard_normal((B, J)))
    wz_words, wz_scales = pack_weight(np.random.standard_normal((Z, H)) / np.sqrt(Z) / sz[:, None], "e4m3")
    wp_words, wp_scales = pack_weight(np.random.standard_normal((Q, H)) / np.sqrt(Q) / np.repeat(su, J)[:, None], "e4m3")
    g = bf((1.0 + 0.1 * np.random.standard_normal(H)) * t)
    w2_words, w2_scales = pack_weight(np.random.standard_normal((H, O)) / np.sqrt(H) / t[:, None], "e4m3")
    return {"z": z,
            "u": u,
            "v": v,
            "wz_words": wz_words,
            "wz_scales": wz_scales,
            "wp_words": wp_words,
            "wp_scales": wp_scales,
            "g": g,
            "w2_words": w2_words,
            "w2_scales": w2_scales}


def core(z, u, v, wz_words, wz_scales, wp_words, wp_scales, g, w2_words, w2_scales):
    p = row_outer(f64(u), f64(v))
    s = (mxq(f64(z), 1, "e4m3") @ unpack_weight(wz_words, wz_scales, "e4m3")) + (mxq(p, 1, "e4m3") @ unpack_weight(wp_words, wp_scales, "e4m3"))
    a = leaky(s)
    ag = a * f64(g)[None, :]
    y = mxq(ag, 1, "e4m3") @ unpack_weight(w2_words, w2_scales, "e4m3")
    return y


def e4m3fn_bytes(y):
    return np.clip(np.asarray(y, np.float64), -448.0, 448.0).astype(np.float32).astype(ml_dtypes.float8_e4m3fn).view(np.uint8)


def e4m3fn_values(b):
    return np.asarray(b, np.uint8).view(ml_dtypes.float8_e4m3fn).astype(np.float64)


def setup_inputs():
    d = draw0()
    x0 = np.asarray(d['z']).astype(np.float64)
    s = (np.max(np.abs(x0), axis=(0,), keepdims=True) / 448.0).astype(np.float32)
    out = {}
    for k, v in d.items():
        if k == 'z':
            out['z_bytes'] = e4m3fn_bytes(x0 / s.astype(np.float64))
            out['z_scale'] = s
        else:
            out[k] = v
    return out


def reference(z_bytes, z_scale, u, v, wz_words, wz_scales, wp_words, wp_scales, g, w2_words, w2_scales):
    return core(e4m3fn_values(z_bytes) * z_scale.astype(np.float64), u, v, wz_words, wz_scales, wp_words, wp_scales, g, w2_words, w2_scales)

@@ -1,0 +1,308 @@
+from contextlib import ExitStack
+
+import concourse.mybir as mybir
+from concourse.masks import make_identity
+
+B, I, J, Z, H, O = 1024, 64, 32, 1024, 1024, 512
+Q = I * J
+FLOPS = 2 * B * (Z + Q) * H + 2 * B * H * O
+
+F32 = mybir.dt.float32
+BF16 = mybir.dt.bfloat16
+I32 = mybir.dt.int32
+U32 = mybir.dt.uint32
+U8 = mybir.dt.uint8
+FP8 = mybir.dt.float8_e4m3fn
+FP8X4 = mybir.dt.float8_e4m3fn_x4
+ALU = mybir.AluOpType
+ACT = mybir.ActivationFunctionType
+
+P = 128
+NT = B // P
+BANK = 512
+ZP = Z // 512
+PP = Q // 512
+HP = H // 512
+
+
+def tile_outerproductpnntwolayer_w8_kernel(
+    tc, z_bytes, z_scale, u, v, wz_words, wz_scales, wp_words, wp_scales, g, w2_words, w2_scales, out
+):
+    nc = tc.nc
+    with ExitStack() as ctx:
+        keep = ctx.enter_context(tc.tile_pool(name="keep", bufs=1))
+        work = ctx.enter_context(tc.tile_pool(name="work", bufs=3))
+        psum = ctx.enter_context(tc.psum_pool(name="psum", bufs=1))
+        ctx.enter_context(tc.manual_schedule())
+
+        ident = keep.tile([P, P], F32, name="ident")
+        make_identity(nc, ident[:])
+
+        wp_sc = keep.tile([P, H], U8, name="wp_sc", align_bytes=64)
+        wz_sc = keep.tile([P, H], U8, name="wz_sc", align_bytes=64)
+        w2_sc = keep.tile([P, O], U8, name="w2_sc", align_bytes=64)
+        for plane in (wp_sc, wz_sc, w2_sc):
+            nc.vector.memset(plane[:].bitcast(I32), 0)
+
+        def load_scales(queue, plane, scales):
+            passes = scales.shape[0]
+            for quad in range(4):
+                queue.dma_start(
+                    out=plane[32 * quad : 32 * quad + 4 * passes, :].bitcast(I32),
+                    in_=scales[:, 4 * quad : 4 * quad + 4, :].bitcast(I32),
+                )
+
+        def load_words(words, c, name):
+            tile = keep.tile([P, words.shape[2]], U32, name=name, align_bytes=64)
+            nc.sync.dma_start(out=tile[:].bitcast(I32), in_=words[c].rearrange("p n t -> p (n t)").bitcast(I32))
+            return tile
+
+        z_rows = z_bytes.rearrange("(p n) k -> p n k", n=NT)
+        out_rows = out.rearrange("(p n) o -> p n o", n=NT)
+        z_raw = {}
+
+        def load_z(pair):
+            tile = keep.tile([P, 2, Z], U8, name="z_raw%d" % pair, align_bytes=64)
+            nc.sync.dma_start(out=tile[:], in_=z_rows[:, 2 * pair : 2 * pair + 2, :])
+            z_raw[pair] = tile
+
+        u_sb = keep.tile([P, NT * I], BF16, name="u_sb")
+        nc.sync.dma_start(out=u_sb[:], in_=u.rearrange("(p n) i -> p (n i)", n=NT))
+        v_sb = keep.tile([P, NT * J], BF16, name="v_sb")
+        nc.sync.dma_start(out=v_sb[:], in_=v.rearrange("(p n) j -> p (n j)", n=NT))
+        load_z(0)
+        zs_sb = keep.tile([P, Z], F32, name="zs_sb")
+        nc.sync.dma_start(out=zs_sb[:], in_=z_scale.rearrange("o k -> (o k)").partition_broadcast(P))
+        load_scales(nc.scalar, wp_sc, wp_scales)
+        wp_w = [load_words(wp_words, c, "wp_w%d" % c) for c in range(PP)]
+        load_z(1)
+        load_scales(nc.sync, wz_sc, wz_scales)
+        wz_w = [load_words(wz_words, c, "wz_w%d" % c) for c in range(ZP)]
+        g_sb = keep.tile([P, H], BF16, name="g_sb")
+        nc.sync.dma_start(out=g_sb[:], in_=g.partition_broadcast(P))
+        load_z(2)
+        load_z(3)
+        load_scales(nc.sync, w2_sc, w2_scales)
+        w2_w = [load_words(w2_words, c, "w2_w%d" % c) for c in range(HP)]
+
+        FIRST = 2
+        u2_a = keep.tile([P, FIRST * I, 2], BF16, name="u2_a")
+        u2_b = keep.tile([P, (NT - FIRST) * I, 2], BF16, name="u2_b")
+        nc.scalar.activation(
+            out=u2_a[:], in_=u_sb[:, : FIRST * I].unsqueeze(2).to_broadcast([P, FIRST * I, 2]), func=ACT.Identity
+        )
+        v_words = v_sb[:].bitcast(F32).rearrange("p (n r u) -> p n u r", n=NT, u=2)
+        v_wide = {}
+
+        def widen_v(engine_copy, pair):
+            tile = work.tile([P, 2, 2, 16, 8], F32, name="v_wide", bufs=2)
+            engine_copy(out=tile[:], in_=v_words[:, 2 * pair : 2 * pair + 2].unsqueeze(3).to_broadcast([P, 2, 2, 16, 8]))
+            v_wide[pair] = tile
+
+        widen_v(nc.vector.tensor_copy, 0)
+        u_wide = {}
+
+        def widen_u(src, first, count):
+            tile = keep.tile([P, count * I, 8], F32, name="u_wide%d" % first)
+            nc.vector.tensor_copy(out=tile[:], in_=src.unsqueeze(2).to_broadcast([P, count * I, 8]))
+            flat = tile[:].rearrange("p c r -> p (c r)")
+            for n in range(count):
+                u_wide[first + n] = flat[:, n * BANK : (n + 1) * BANK]
+
+        u2_a_words = u2_a[:].rearrange("p c e -> p (c e)").bitcast(F32)
+        widen_u(u2_a_words[:, :I], 0, 1)
+        widen_u(u2_a_words[:, I:], 1, 1)
+        nc.vector.tensor_copy(out=u2_b[:], in_=u_sb[:, FIRST * I :].unsqueeze(2).to_broadcast([P, (NT - FIRST) * I, 2]))
+        widen_u(u2_b[:].rearrange("p c e -> p (c e)").bitcast(F32), FIRST, NT - FIRST)
+
+        v_bank, v_t = {}, {}
+        u_bank, z_bank, a_bank, o_bank = {}, {}, {}, {}
+        z_bf, z_t, p_t, a_t = {}, {}, {}, {}
+        z_q, p_q, a_q = {}, {}, {}
+        acc, sgn, fac, y_bf, a_bf = {}, {}, {}, {}, {}
+
+        def turn_v(pair):
+            bank = psum.tile([P, 2, 2, P], F32, name="v_bank", tag="a_bank")
+            src = v_wide[pair][:].rearrange("p n u q r -> p n u (q r)")
+            for n in range(2):
+                for w in range(2):
+                    nc.tensor.transpose(bank[:, n, w, :], src[:, n, w, :], ident[:])
+            v_bank[pair] = bank
+
+        def empty_v(pair):
+            tile = keep.tile([P, 2, P, 2], F32, name="v_t%d" % pair)
+            nc.scalar.copy(out=tile[:], in_=v_bank[pair][:].rearrange("p n u b -> p n b u"))
+            for n in range(2):
+                v_t[2 * pair + n] = tile[:, n].rearrange("p b u -> p (b u)").bitcast(BF16)
+
+        def scale_z(n):
+            tile = work.tile([P, Z], BF16, name="z_bf", align_bytes=64)
+            nc.vector.tensor_tensor(out=tile[:], in0=z_raw[n // 2][:, n % 2, :].bitcast(FP8), in1=zs_sb[:], op=ALU.mult)
+            z_bf[n] = tile
+
+        def turn_u(n):
+            bank = psum.tile([P, PP, P], F32, name="u_bank")
+            for c in range(PP):
+                nc.tensor.transpose(bank[:, c, :], u_wide[n][:, c * P : (c + 1) * P], ident[:])
+            u_bank[n] = bank
+
+        def turn_z(n):
+            bank = psum.tile([P, ZP, 2, P], F32, name="z_bank")
+            words = z_bf[n][:].bitcast(F32)
+            for c in range(ZP):
+                for w in range(2):
+                    nc.tensor.transpose(bank[:, c, w, :], words[:, 256 * c + w : 256 * (c + 1) : 2], ident[:])
+            z_bank[n] = bank
+
+        def turn_a(n):
+            bank = psum.tile([P, HP, 2, P], F32, name="a_bank")
+            words = a_bf[n][:].bitcast(F32)
+            for c in range(HP):
+                for w in range(2):
+                    nc.tensor.transpose(bank[:, c, w, :], words[:, P * (2 * c + w) : P * (2 * c + w + 1)], ident[:])
+            a_bank[n] = bank
+
+        def empty_words(bank, name):
+            tile = work.tile([P, 2 * BANK], BF16, name=name, align_bytes=64)
+            nc.scalar.copy(
+                out=tile[:].bitcast(F32).rearrange("p (c b u) -> p c b u", c=2, u=2),
+                in_=bank[:].rearrange("p c u b -> p c b u"),
+            )
+            return tile
+
+        def outer(n):
+            tile = work.tile([P, Q], BF16, name="p_t", align_bytes=64)
+            shape = [P, PP, P, 2, 2]
+            u_pairs = u_bank[n][:].rearrange("p c b -> p (c b)").bitcast(BF16).rearrange("p (c b e) -> p c b e", c=PP, e=2)
+            nc.vector.tensor_tensor(
+                out=tile[:].rearrange("p (c b u e) -> p c b u e", c=PP, u=2, e=2),
+                in0=u_pairs.unsqueeze(3).to_broadcast(shape),
+                in1=v_t[n].rearrange("p (b u e) -> p b u e", u=2, e=2).unsqueeze(1).to_broadcast(shape),
+                op=ALU.mult,
+            )
+            p_t[n] = tile
+
+        def quantize(src, name):
+            width = src.shape[1] // 4
+            codes = work.tile([P, width], U32, name=name + "_codes", align_bytes=64)
+            scales = work.tile([P, width], U8, name=name + "_scales", align_bytes=64)
+            nc.vector.quantize_mx(out=codes[:].bitcast(FP8X4), scales=scales[:], in_=src[:])
+            return codes, scales
+
+        def mx_pass(bank, act, c, w_words, w_scales, cols, start, stop):
+            codes, scales = act
+            nc.tensor.matmul_mx(
+                out=bank[:],
+                lhsT=codes[:, c * P : (c + 1) * P].bitcast(FP8X4),
+                lhsT_scale=scales[:, c * P : (c + 1) * P],
+                rhs=w_words[c][:, cols].bitcast(FP8X4),
+                rhs_scale=w_scales[4 * c :, cols],
+                start=start,
+                stop=stop,
+            )
+
+        def layer1_pass(n, half, j):
+            cols = slice(half * BANK, (half + 1) * BANK)
+            if j == 0:
+                acc[n, half] = psum.tile([P, BANK], F32, name="acc%d" % half, bufs=2)
+            if j < PP:
+                mx_pass(acc[n, half], p_q[n], j, wp_w, wp_sc, cols, j == 0, False)
+            else:
+                mx_pass(acc[n, half], z_q[n], j - PP, wz_w, wz_sc, cols, False, j == PP + ZP - 1)
+
+        def by_word(ap):
+            return ap.rearrange("p (m u e) -> p u m e", u=2, e=2)
+
+        def in_order(ap):
+            return ap.rearrange("p (u m e) -> p u m e", u=2, e=2)
+
+        def sign_s(n, half):
+            tile = work.tile([P, BANK], BF16, name="sgn")
+            nc.scalar.activation(out=in_order(tile[:]), in_=by_word(acc[n, half][:]), func=ACT.Sign)
+            sgn[n, half] = tile
+
+        def slope(n, half):
+            if half == 0:
+                fac[n] = work.tile([P, H], BF16, name="fac")
+            nc.scalar.activation(
+                out=fac[n][:, half * BANK : (half + 1) * BANK], in_=sgn[n, half][:], func=ACT.Identity, scale=0.375, bias=0.625
+            )
+
+        def gain(n, half):
+            cols = slice(half * BANK, (half + 1) * BANK)
+            if half == 0:
+                y_bf[n] = work.tile([P, H], BF16, name="y_bf")
+            nc.vector.tensor_tensor(
+                out=in_order(y_bf[n][:, cols]), in0=by_word(acc[n, half][:]), in1=by_word(g_sb[:, cols]), op=ALU.mult
+            )
+
+        def rectify(n):
+            tile = work.tile([P, H], BF16, name="a_bf")
+            nc.vector.tensor_tensor(out=tile[:], in0=y_bf[n][:], in1=fac[n][:], op=ALU.mult)
+            a_bf[n] = tile
+
+        def layer2(n):
+            bank = psum.tile([P, O], F32, name="o_bank")
+            for c in range(HP):
+                mx_pass(bank, a_q[n], c, w2_w, w2_sc, slice(0, O), c == 0, c == HP - 1)
+            o_bank[n] = bank
+
+        def store(n):
+            tile = work.tile([P, O], F32, name="o_sb")
+            nc.scalar.copy(out=tile[:], in_=o_bank[n][:])
+            nc.sync.dma_start(out=out_rows[:, n, :], in_=tile[:])
+
+        def live(n):
+            return 0 <= n < NT
+
+        for k in range(-2, NT + 3):
+            pair = k + 2
+            if live(k - 1):
+                slope(k - 1, 1)
+                gain(k - 1, 1)
+            if 0 < pair < NT // 2:
+                widen_v(nc.scalar.copy, pair)
+            if pair < NT // 2:
+                turn_v(pair)
+            if live(k + 1):
+                turn_u(k + 1)
+                turn_z(k + 1)
+            if live(k - 2):
+                turn_a(k - 2)
+            if live(k + 1):
+                outer(k + 1)
+                z_t[k + 1] = empty_words(z_bank[k + 1], "z_t")
+            if pair < NT // 2:
+                empty_v(pair)
+            if live(k - 2):
+                a_t[k - 2] = empty_words(a_bank[k - 2], "a_t")
+            if live(k - 3):
+                store(k - 3)
+            if live(k - 1):
+                rectify(k - 1)
+            if live(k + 1):
+                z_q[k + 1] = quantize(z_t[k + 1], "z")
+            if live(k - 2):
+                a_q[k - 2] = quantize(a_t[k - 2], "a")
+            if live(k + 1):
+                p_q[k + 1] = quantize(p_t[k + 1], "p")
+            if live(k + 2):
+                scale_z(k + 2)
+            if k == 0:
+                for j in range(PP + ZP):
+                    for half in range(2):
+                        layer1_pass(k, half, j)
+            elif live(k):
+                for j in range(PP + ZP):
+                    layer1_pass(k, 0, j)
+            if live(k):
+                sign_s(k, 0)
+                slope(k, 0)
+                gain(k, 0)
+            if live(k) and k > 0:
+                for j in range(PP + ZP):
+                    layer1_pass(k, 1, j)
+            if live(k - 2):
+                layer2(k - 2)
+            if live(k):
+                sign_s(k, 1)

@@ -18,11 +18,17 @@ ALU = mybir.AluOpType
 ACT = mybir.ActivationFunctionType
 
 P = 128
-NT = B // P
+TILES = B // P
+LAST = TILES - 1
 BANK = 512
-ZP = Z // 512
-PP = Q // 512
-HP = H // 512
+K_PASS = 512
+Z_PASSES, P_PASSES, A_PASSES = Z // K_PASS, Q // K_PASS, H // K_PASS
+BLOCKS = 16
+BLOCK_ROWS = 8
+QUARTER = BANK // 2
+NEAR = 3
+LAG = 3
+SMALL_BANKS = 4
 
 
 def tile_outerproductpnntwolayer_w8_kernel(
@@ -35,30 +41,33 @@ def tile_outerproductpnntwolayer_w8_kernel(
         psum = ctx.enter_context(tc.psum_pool(name="psum", bufs=1))
         ctx.enter_context(tc.manual_schedule())
 
+        def psum_bank(shape, name, tag="small"):
+            return psum.tile(shape, F32, name=name, tag=tag, bufs=SMALL_BANKS if tag == "small" else 2)
+
         ident = keep.tile([P, P], F32, name="ident")
         make_identity(nc, ident[:])
 
         wp_sc = keep.tile([P, H], U8, name="wp_sc", align_bytes=64)
         wz_sc = keep.tile([P, H], U8, name="wz_sc", align_bytes=64)
         w2_sc = keep.tile([P, O], U8, name="w2_sc", align_bytes=64)
-        for plane in (wp_sc, wz_sc, w2_sc):
-            nc.vector.memset(plane[:].bitcast(I32), 0)
+        for scale_tile in (wp_sc, wz_sc, w2_sc):
+            nc.vector.memset(scale_tile[:].bitcast(I32), 0)
 
-        def load_scales(queue, plane, scales):
+        def load_scales(queue, scale_tile, scales):
             passes = scales.shape[0]
             for quad in range(4):
                 queue.dma_start(
-                    out=plane[32 * quad : 32 * quad + 4 * passes, :].bitcast(I32),
+                    out=scale_tile[32 * quad : 32 * quad + 4 * passes, :].bitcast(I32),
                     in_=scales[:, 4 * quad : 4 * quad + 4, :].bitcast(I32),
                 )
 
-        def load_words(words, c, name):
-            tile = keep.tile([P, words.shape[2]], U32, name=name, align_bytes=64)
-            nc.sync.dma_start(out=tile[:].bitcast(I32), in_=words[c].rearrange("p n t -> p (n t)").bitcast(I32))
+        def load_codes(codes, c, name):
+            tile = keep.tile([P, codes.shape[2]], U32, name=name, align_bytes=64)
+            nc.sync.dma_start(out=tile[:].bitcast(I32), in_=codes[c].rearrange("p n t -> p (n t)").bitcast(I32))
             return tile
 
-        z_rows = z_bytes.rearrange("(p n) k -> p n k", n=NT)
-        out_rows = out.rearrange("(p n) o -> p n o", n=NT)
+        z_rows = z_bytes.rearrange("(b n) k -> b n k", n=TILES)
+        out_rows = out.rearrange("(b n) o -> b n o", n=TILES)
         z_raw = {}
 
         def load_z(pair):
@@ -66,243 +75,460 @@ def tile_outerproductpnntwolayer_w8_kernel(
             nc.sync.dma_start(out=tile[:], in_=z_rows[:, 2 * pair : 2 * pair + 2, :])
             z_raw[pair] = tile
 
-        u_sb = keep.tile([P, NT * I], BF16, name="u_sb")
-        nc.sync.dma_start(out=u_sb[:], in_=u.rearrange("(p n) i -> p (n i)", n=NT))
-        v_sb = keep.tile([P, NT * J], BF16, name="v_sb")
-        nc.sync.dma_start(out=v_sb[:], in_=v.rearrange("(p n) j -> p (n j)", n=NT))
-        load_z(0)
-        zs_sb = keep.tile([P, Z], F32, name="zs_sb")
-        nc.sync.dma_start(out=zs_sb[:], in_=z_scale.rearrange("o k -> (o k)").partition_broadcast(P))
+        u_sb = keep.tile([P, TILES * I], BF16, name="u_sb")
+        nc.sync.dma_start(out=u_sb[:], in_=u.rearrange("(b n) i -> b (n i)", n=TILES))
+        v_sb = keep.tile([P, TILES * J], BF16, name="v_sb")
+        nc.sync.dma_start(out=v_sb[:], in_=v.rearrange("(b n) j -> b (n j)", n=TILES))
+        zs_per_row = Z // P
+        zs_rows = keep.tile([P, zs_per_row], F32, name="zs_rows")
+        nc.sync.dma_start(out=zs_rows[:], in_=z_scale.rearrange("o (a m) -> a (o m)", a=P))
         load_scales(nc.scalar, wp_sc, wp_scales)
-        wp_w = [load_words(wp_words, c, "wp_w%d" % c) for c in range(PP)]
-        load_z(1)
-        load_scales(nc.sync, wz_sc, wz_scales)
-        wz_w = [load_words(wz_words, c, "wz_w%d" % c) for c in range(ZP)]
-        g_sb = keep.tile([P, H], BF16, name="g_sb")
-        nc.sync.dma_start(out=g_sb[:], in_=g.partition_broadcast(P))
-        load_z(2)
-        load_z(3)
-        load_scales(nc.sync, w2_sc, w2_scales)
-        w2_w = [load_words(w2_words, c, "w2_w%d" % c) for c in range(HP)]
+        wp_sb = [load_codes(wp_words, c, "wp_sb%d" % c) for c in range(2)]
+        load_z(0)
+        wp_sb.extend(load_codes(wp_words, c, "wp_sb%d" % c) for c in range(2, P_PASSES))
 
-        FIRST = 2
-        u2_a = keep.tile([P, FIRST * I, 2], BF16, name="u2_a")
-        u2_b = keep.tile([P, (NT - FIRST) * I, 2], BF16, name="u2_b")
-        nc.scalar.activation(
-            out=u2_a[:], in_=u_sb[:, : FIRST * I].unsqueeze(2).to_broadcast([P, FIRST * I, 2]), func=ACT.Identity
-        )
-        v_words = v_sb[:].bitcast(F32).rearrange("p (n r u) -> p n u r", n=NT, u=2)
-        v_wide = {}
+        v_words = v_sb[:].bitcast(F32).rearrange("b (n r w) -> b n w r", n=TILES, w=2)
+        u_doubled, u_wide, v_wide, u_by_pass = {}, {}, {}, {}
+        u_bank, u_far, v_bank, v_t = {}, {}, {}, {}
 
-        def widen_v(engine_copy, pair):
-            tile = work.tile([P, 2, 2, 16, 8], F32, name="v_wide", bufs=2)
-            engine_copy(out=tile[:], in_=v_words[:, 2 * pair : 2 * pair + 2].unsqueeze(3).to_broadcast([P, 2, 2, 16, 8]))
-            v_wide[pair] = tile
-
-        widen_v(nc.vector.tensor_copy, 0)
-        u_wide = {}
-
-        def widen_u(src, first, count):
-            tile = keep.tile([P, count * I, 8], F32, name="u_wide%d" % first)
-            nc.vector.tensor_copy(out=tile[:], in_=src.unsqueeze(2).to_broadcast([P, count * I, 8]))
-            flat = tile[:].rearrange("p c r -> p (c r)")
+        def double_u(first, count):
+            tile = keep.tile([P, count * I, 2], BF16, name="u_doubled%d" % first)
+            nc.scalar.activation(
+                out=tile[:],
+                in_=u_sb[:, first * I : (first + count) * I].unsqueeze(2).to_broadcast([P, count * I, 2]),
+                func=ACT.Identity,
+            )
+            words = tile[:].rearrange("b i e -> b (i e)").bitcast(F32)
             for n in range(count):
-                u_wide[first + n] = flat[:, n * BANK : (n + 1) * BANK]
+                u_doubled[first + n] = words[:, n * I : (n + 1) * I]
 
-        u2_a_words = u2_a[:].rearrange("p c e -> p (c e)").bitcast(F32)
-        widen_u(u2_a_words[:, :I], 0, 1)
-        widen_u(u2_a_words[:, I:], 1, 1)
-        nc.vector.tensor_copy(out=u2_b[:], in_=u_sb[:, FIRST * I :].unsqueeze(2).to_broadcast([P, (NT - FIRST) * I, 2]))
-        widen_u(u2_b[:].rearrange("p c e -> p (c e)").bitcast(F32), FIRST, NT - FIRST)
-
-        v_bank, v_t = {}, {}
-        u_bank, z_bank, a_bank, o_bank = {}, {}, {}, {}
-        z_bf, z_t, p_t, a_t = {}, {}, {}, {}
-        z_q, p_q, a_q = {}, {}, {}
-        acc, sgn, fac, y_bf, a_bf = {}, {}, {}, {}, {}
-
-        def turn_v(pair):
-            bank = psum.tile([P, 2, 2, P], F32, name="v_bank", tag="a_bank")
-            src = v_wide[pair][:].rearrange("p n u q r -> p n u (q r)")
-            for n in range(2):
-                for w in range(2):
-                    nc.tensor.transpose(bank[:, n, w, :], src[:, n, w, :], ident[:])
-            v_bank[pair] = bank
-
-        def empty_v(pair):
-            tile = keep.tile([P, 2, P, 2], F32, name="v_t%d" % pair)
-            nc.scalar.copy(out=tile[:], in_=v_bank[pair][:].rearrange("p n u b -> p n b u"))
-            for n in range(2):
-                v_t[2 * pair + n] = tile[:, n].rearrange("p b u -> p (b u)").bitcast(BF16)
-
-        def scale_z(n):
-            tile = work.tile([P, Z], BF16, name="z_bf", align_bytes=64)
-            nc.vector.tensor_tensor(out=tile[:], in0=z_raw[n // 2][:, n % 2, :].bitcast(FP8), in1=zs_sb[:], op=ALU.mult)
-            z_bf[n] = tile
+        def widen_u(engine_copy, n):
+            tile = work.tile([P, I, BLOCK_ROWS], F32, name="u_wide", bufs=TILES)
+            engine_copy(out=tile[:], in_=u_doubled[n].unsqueeze(2).to_broadcast([P, I, BLOCK_ROWS]))
+            u_wide[n] = tile[:].rearrange("b i r -> b (i r)")
 
         def turn_u(n):
-            bank = psum.tile([P, PP, P], F32, name="u_bank")
-            for c in range(PP):
+            bank = psum_bank([P, P_PASSES, P], "u_bank")
+            for c in range(P_PASSES):
                 nc.tensor.transpose(bank[:, c, :], u_wide[n][:, c * P : (c + 1) * P], ident[:])
             u_bank[n] = bank
 
-        def turn_z(n):
-            bank = psum.tile([P, ZP, 2, P], F32, name="z_bank")
-            words = z_bf[n][:].bitcast(F32)
-            for c in range(ZP):
+        def double_u_by_pass(first):
+            shape = [P, 2, TILES, BLOCKS, 2]
+            tile = keep.tile(shape, BF16, name="u_by_pass%d" % first)
+            columns = u_sb[:].rearrange("b (n c q) -> b c n q", n=TILES, c=P_PASSES)[:, first : first + 2]
+            nc.scalar.copy(out=tile[:], in_=columns.unsqueeze(4).to_broadcast(shape))
+            words = tile[:].rearrange("b c n q e -> b (c n q e)").bitcast(F32)
+            for j in range(2):
+                u_by_pass[first + j] = words[:, j * P : (j + 1) * P]
+
+        parked = out_rows[:, LAST, :]
+
+        def park_u():
+            bank = psum_bank([P, P_PASSES, P], "park_bank")
+            for c in range(P_PASSES):
+                nc.tensor.transpose(bank[:, c, :], u_by_pass[c], ident[:])
+            rows = keep.tile([P, BANK], F32, name="u_rows")
+            nc.scalar.copy(out=rows[:], in_=bank[:].rearrange("p c b -> p (c b)"))
+            nc.sync.dma_start(out=parked[BLOCKS * NEAR :, :], in_=rows[BLOCKS * NEAR :, :])
+
+        def fetch_u(n):
+            tile = keep.tile([P, BANK], F32, name="u_far%d" % n)
+            rows = parked[BLOCKS * n : BLOCKS * (n + 1), :]
+            nc.sync.dma_start(out=tile[:], in_=rows.unsqueeze(1).to_broadcast([BLOCKS, BLOCK_ROWS, BANK]))
+            u_far[n] = tile
+
+        def widen_v(engine_copy, first, count):
+            shape = [P, count, 2, BLOCKS, BLOCK_ROWS]
+            tile = keep.tile(shape, F32, name="v_wide%d" % first)
+            engine_copy(out=tile[:], in_=v_words[:, first : first + count].unsqueeze(3).to_broadcast(shape))
+            for j in range(count):
+                v_wide[first + j] = tile[:, j].rearrange("b w q r -> b w (q r)")
+
+        def turn_v(first, count):
+            bank = psum_bank([P, count, 2, P], "v_bank")
+            for j in range(count):
                 for w in range(2):
-                    nc.tensor.transpose(bank[:, c, w, :], words[:, 256 * c + w : 256 * (c + 1) : 2], ident[:])
+                    nc.tensor.transpose(bank[:, j, w, :], v_wide[first + j][:, w, :], ident[:])
+            v_bank[first] = bank
+
+        def empty_v(first):
+            count = v_bank[first].shape[1]
+            tile = keep.tile([P, count, P, 2], F32, name="v_t%d" % first)
+            nc.scalar.copy(out=tile[:], in_=v_bank[first][:].rearrange("p n w b -> p n b w"))
+            for j in range(count):
+                v_t[first + j] = tile[:, j].rearrange("p b w -> p (b w)").bitcast(BF16)
+
+        double_u(0, 1)
+        double_u(1, NEAR - 1)
+        load_z(1)
+        load_scales(nc.sync, wz_sc, wz_scales)
+        wz_sb = [load_codes(wz_words, c, "wz_sb%d" % c) for c in range(Z_PASSES)]
+        load_z(2)
+        g_sb = keep.tile([P, H], BF16, name="g_sb")
+        w2_sb = []
+
+        def late_loads():
+            nc.sync.dma_start(out=g_sb[:], in_=g.partition_broadcast(P))
+            fetch_u(NEAR)
+            load_z(3)
+            for n in range(NEAR + 1, TILES):
+                fetch_u(n)
+            load_scales(nc.sync, w2_sc, w2_scales)
+            w2_sb.extend(load_codes(w2_words, c, "w2_sb%d" % c) for c in range(A_PASSES))
+
+        zs_sb = keep.tile([P, Z], F32, name="zs_sb")
+        z_bf, z_sorted, z_bank, z_t = {}, {}, {}, {}
+
+        def spread_z_scale(half, tag):
+            count = zs_per_row // 2
+            columns = zs_sb[:].rearrange("b (a m) -> b a m", m=zs_per_row)
+            bank = psum_bank([P, count, P], "zs_bank", tag)
+            for j in range(count):
+                m = count * half + j
+                nc.tensor.transpose(bank[:, j, :], zs_rows[:, m : m + 1].to_broadcast([P, P]), ident[:])
+            nc.scalar.copy(out=columns[:, :, count * half : count * (half + 1)], in_=bank[:].rearrange("b j a -> b a j"))
+
+        def scale_z(n):
+            tile = work.tile([P, Z], BF16, name="z_bf", align_bytes=64, bufs=5)
+            nc.vector.tensor_tensor(out=tile[:], in0=z_raw[n // 2][:, n % 2, :].bitcast(FP8), in1=zs_sb[:], op=ALU.mult)
+            z_bf[n] = tile
+
+        def sort_z(n):
+            tile = work.tile([P, Z_PASSES, 2, P], F32, name="z_sorted")
+            nc.scalar.copy(out=tile[:], in_=z_bf[n][:].bitcast(F32).rearrange("b (c p w) -> b c w p", c=Z_PASSES, w=2))
+            z_sorted[n] = tile
+
+        def turn_z(n):
+            bank = psum_bank([P, Z_PASSES, 2, P], "z_bank")
+            words = z_bf[n][:].bitcast(F32)
+            for c in range(Z_PASSES):
+                for w in range(2):
+                    if n in z_sorted:
+                        source = z_sorted[n][:, c, w, :]
+                    else:
+                        source = words[:, 2 * P * c + w : 2 * P * (c + 1) : 2]
+                    nc.tensor.transpose(bank[:, c, w, :], source, ident[:])
             z_bank[n] = bank
 
-        def turn_a(n):
-            bank = psum.tile([P, HP, 2, P], F32, name="a_bank")
-            words = a_bf[n][:].bitcast(F32)
-            for c in range(HP):
-                for w in range(2):
-                    nc.tensor.transpose(bank[:, c, w, :], words[:, P * (2 * c + w) : P * (2 * c + w + 1)], ident[:])
-            a_bank[n] = bank
-
         def empty_words(bank, name):
-            tile = work.tile([P, 2 * BANK], BF16, name=name, align_bytes=64)
+            count = bank.shape[1]
+            tile = work.tile([P, count * K_PASS], BF16, name=name, align_bytes=64)
             nc.scalar.copy(
-                out=tile[:].bitcast(F32).rearrange("p (c b u) -> p c b u", c=2, u=2),
-                in_=bank[:].rearrange("p c u b -> p c b u"),
+                out=tile[:].bitcast(F32).rearrange("p (c b w) -> p c b w", c=count, w=2),
+                in_=bank[:].rearrange("p c w b -> p c b w"),
             )
             return tile
 
-        def outer(n):
-            tile = work.tile([P, Q], BF16, name="p_t", align_bytes=64)
-            shape = [P, PP, P, 2, 2]
-            u_pairs = u_bank[n][:].rearrange("p c b -> p (c b)").bitcast(BF16).rearrange("p (c b e) -> p c b e", c=PP, e=2)
+        def empty_z(n):
+            z_t[n] = empty_words(z_bank[n], "z_t")
+
+        p_t = {}
+
+        def outer(n, first=0, count=P_PASSES):
+            tile = work.tile([P, count * K_PASS], BF16, name="p_t", align_bytes=64, bufs=4)
+            shape = [P, count, P, 2, 2]
+            u_words = u_far[n][:] if n >= NEAR else u_bank[n][:].rearrange("p c b -> p (c b)")
+            u_twice = u_words.bitcast(BF16).rearrange("p (c b e) -> p c b e", c=P_PASSES, e=2)
             nc.vector.tensor_tensor(
-                out=tile[:].rearrange("p (c b u e) -> p c b u e", c=PP, u=2, e=2),
-                in0=u_pairs.unsqueeze(3).to_broadcast(shape),
-                in1=v_t[n].rearrange("p (b u e) -> p b u e", u=2, e=2).unsqueeze(1).to_broadcast(shape),
+                out=tile[:].rearrange("p (c b w e) -> p c b w e", c=count, w=2, e=2),
+                in0=u_twice[:, first : first + count].unsqueeze(3).to_broadcast(shape),
+                in1=v_t[n].rearrange("p (b w e) -> p b w e", w=2, e=2).unsqueeze(1).to_broadcast(shape),
                 op=ALU.mult,
             )
-            p_t[n] = tile
+            p_t[n, first] = tile
 
-        def quantize(src, name):
-            width = src.shape[1] // 4
-            codes = work.tile([P, width], U32, name=name + "_codes", align_bytes=64)
-            scales = work.tile([P, width], U8, name=name + "_scales", align_bytes=64)
-            nc.vector.quantize_mx(out=codes[:].bitcast(FP8X4), scales=scales[:], in_=src[:])
-            return codes, scales
+        z_q, p_q, a_q = {}, {}, {}
+        a_t = {}
 
-        def mx_pass(bank, act, c, w_words, w_scales, cols, start, stop):
-            codes, scales = act
+        def quantize(source, name, into, n, first):
+            width = source.shape[1] // 4
+            codes = work.tile([P, width], U32, name=name + "_codes", align_bytes=64, bufs=4)
+            scales = work.tile([P, width], U8, name=name + "_scales", align_bytes=64, bufs=4)
+            nc.vector.quantize_mx(out=codes[:].bitcast(FP8X4), scales=scales[:], in_=source[:])
+            for c in range(width // P):
+                into[n, first + c] = (codes[:, c * P : (c + 1) * P], scales[:, c * P : (c + 1) * P])
+
+        def quantize_p(n, first=0):
+            quantize(p_t[n, first], "p", p_q, n, first)
+
+        def quantize_z(n):
+            quantize(z_t[n], "z", z_q, n, 0)
+
+        def quantize_a(n, first=0):
+            quantize(a_t[n, first], "a", a_q, n, first)
+
+        def mx_pass(bank, tokens, c, weight, weight_scales, cols, start, stop):
+            codes, scales = tokens
             nc.tensor.matmul_mx(
                 out=bank[:],
-                lhsT=codes[:, c * P : (c + 1) * P].bitcast(FP8X4),
-                lhsT_scale=scales[:, c * P : (c + 1) * P],
-                rhs=w_words[c][:, cols].bitcast(FP8X4),
-                rhs_scale=w_scales[4 * c :, cols],
+                lhsT=codes.bitcast(FP8X4),
+                lhsT_scale=scales,
+                rhs=weight[c][:, cols].bitcast(FP8X4),
+                rhs_scale=weight_scales[4 * c :, cols],
                 start=start,
                 stop=stop,
             )
 
-        def layer1_pass(n, half, j):
-            cols = slice(half * BANK, (half + 1) * BANK)
-            if j == 0:
-                acc[n, half] = psum.tile([P, BANK], F32, name="acc%d" % half, bufs=2)
-            if j < PP:
-                mx_pass(acc[n, half], p_q[n], j, wp_w, wp_sc, cols, j == 0, False)
+        sums = {}
+        layer1_passes = range(P_PASSES + Z_PASSES)
+        z_part = layer1_passes[P_PASSES:]
+
+        def layer1_pass(bank, n, cols, j):
+            if j < P_PASSES:
+                mx_pass(bank, p_q[n, j], j, wp_sb, wp_sc, cols, j == 0, False)
             else:
-                mx_pass(acc[n, half], z_q[n], j - PP, wz_w, wz_sc, cols, False, j == PP + ZP - 1)
+                mx_pass(bank, z_q[n, j - P_PASSES], j - P_PASSES, wz_sb, wz_sc, cols, False, j == layer1_passes[-1])
 
-        def by_word(ap):
-            return ap.rearrange("p (m u e) -> p u m e", u=2, e=2)
+        def one_half(n, half, passes=layer1_passes):
+            for j in passes:
+                if j == 0:
+                    sums[n, half] = psum_bank([P, BANK], "sums", "sums%d" % half)
+                layer1_pass(sums[n, half], n, slice(half * BANK, (half + 1) * BANK), j)
 
-        def in_order(ap):
-            return ap.rearrange("p (u m e) -> p u m e", u=2, e=2)
+        def both_halves(n, passes):
+            for j in passes:
+                for half in range(2):
+                    one_half(n, half, [j])
 
-        def sign_s(n, half):
-            tile = work.tile([P, BANK], BF16, name="sgn")
-            nc.scalar.activation(out=in_order(tile[:]), in_=by_word(acc[n, half][:]), func=ACT.Sign)
-            sgn[n, half] = tile
+        signs, slopes, gained, a_bf, a_bank = {}, {}, {}, {}, {}
 
-        def slope(n, half):
+        def by_word(natural):
+            return natural.rearrange("b (p w e) -> b w p e", w=2, e=2)
+
+        def in_order(sorted_cols):
+            return sorted_cols.rearrange("b (w p e) -> b w p e", w=2, e=2)
+
+        def sign_of_sums(n, half):
+            tile = work.tile([P, BANK], BF16, name="signs", bufs=4)
+            nc.scalar.activation(out=in_order(tile[:]), in_=by_word(sums[n, half][:]), func=ACT.Sign)
+            signs[n, half] = tile
+
+        def slope_from_signs(n, half):
             if half == 0:
-                fac[n] = work.tile([P, H], BF16, name="fac")
+                slopes[n] = work.tile([P, H], BF16, name="slopes")
             nc.scalar.activation(
-                out=fac[n][:, half * BANK : (half + 1) * BANK], in_=sgn[n, half][:], func=ACT.Identity, scale=0.375, bias=0.625
+                out=slopes[n][:, half * BANK : (half + 1) * BANK],
+                in_=signs[n, half][:],
+                func=ACT.Identity,
+                scale=0.375,
+                bias=0.625,
             )
+
+        def slope_from_sums(slope_view, sums_view):
+            nc.vector.tensor_scalar(out=slope_view, in0=sums_view, scalar1=0.0, scalar2=0.25, op0=ALU.is_ge, op1=ALU.max)
 
         def gain(n, half):
             cols = slice(half * BANK, (half + 1) * BANK)
             if half == 0:
-                y_bf[n] = work.tile([P, H], BF16, name="y_bf")
+                gained[n] = work.tile([P, H], BF16, name="gained")
             nc.vector.tensor_tensor(
-                out=in_order(y_bf[n][:, cols]), in0=by_word(acc[n, half][:]), in1=by_word(g_sb[:, cols]), op=ALU.mult
+                out=in_order(gained[n][:, cols]), in0=by_word(sums[n, half][:]), in1=by_word(g_sb[:, cols]), op=ALU.mult
             )
 
-        def rectify(n):
-            tile = work.tile([P, H], BF16, name="a_bf")
-            nc.vector.tensor_tensor(out=tile[:], in0=y_bf[n][:], in1=fac[n][:], op=ALU.mult)
-            a_bf[n] = tile
+        def rectify(n, first=0, count=A_PASSES):
+            cols = slice(first * K_PASS, (first + count) * K_PASS)
+            tile = work.tile([P, count * K_PASS], BF16, name="a_bf", bufs=6)
+            nc.vector.tensor_tensor(out=tile[:], in0=gained[n][:, cols], in1=slopes[n][:, cols], op=ALU.mult)
+            a_bf[n, first] = tile
+
+        def turn_a(n, first=0, count=A_PASSES, tag="small"):
+            bank = psum_bank([P, count, 2, P], "a_bank", tag)
+            words = a_bf[n, first][:].bitcast(F32)
+            for c in range(count):
+                for w in range(2):
+                    nc.tensor.transpose(bank[:, c, w, :], words[:, P * (2 * c + w) : P * (2 * c + w + 1)], ident[:])
+            a_bank[n, first] = bank
+
+        def empty_a(n, first=0):
+            a_t[n, first] = empty_words(a_bank[n, first], "a_t")
+
+        o_bank = {}
 
         def layer2(n):
-            bank = psum.tile([P, O], F32, name="o_bank")
-            for c in range(HP):
-                mx_pass(bank, a_q[n], c, w2_w, w2_sc, slice(0, O), c == 0, c == HP - 1)
-            o_bank[n] = bank
+            o_bank[n] = psum_bank([P, O], "o_bank")
+            for c in range(A_PASSES):
+                mx_pass(o_bank[n], a_q[n, c], c, w2_sb, w2_sc, slice(0, O), c == 0, c == A_PASSES - 1)
 
-        def store(n):
-            tile = work.tile([P, O], F32, name="o_sb")
-            nc.scalar.copy(out=tile[:], in_=o_bank[n][:])
+        def store(n, engine_copy=nc.scalar.copy):
+            tile = work.tile([P, O], F32, name="o_sb", bufs=4)
+            engine_copy(out=tile[:], in_=o_bank[n][:])
             nc.sync.dma_start(out=out_rows[:, n, :], in_=tile[:])
 
-        def live(n):
-            return 0 <= n < NT
+        last_sums, last_out = {}, {}
 
-        for k in range(-2, NT + 3):
-            pair = k + 2
-            if live(k - 1):
-                slope(k - 1, 1)
-                gain(k - 1, 1)
-            if 0 < pair < NT // 2:
-                widen_v(nc.scalar.copy, pair)
-            if pair < NT // 2:
-                turn_v(pair)
-            if live(k + 1):
-                turn_u(k + 1)
-                turn_z(k + 1)
-            if live(k - 2):
-                turn_a(k - 2)
-            if live(k + 1):
-                outer(k + 1)
-                z_t[k + 1] = empty_words(z_bank[k + 1], "z_t")
-            if pair < NT // 2:
-                empty_v(pair)
-            if live(k - 2):
-                a_t[k - 2] = empty_words(a_bank[k - 2], "a_t")
-            if live(k - 3):
-                store(k - 3)
-            if live(k - 1):
+        def last_layer1(part, tag):
+            last_sums[part] = psum_bank([P, QUARTER], "last_sums", tag)
+            for j in layer1_passes:
+                layer1_pass(last_sums[part], LAST, slice(BANK + part * QUARTER, BANK + (part + 1) * QUARTER), j)
+
+        def last_gain_and_slope(part):
+            rows = slice(part * P // 2, (part + 1) * P // 2)
+            sums_view = by_word(last_sums[part][:])
+            gains = by_word(g_sb[:, BANK + part * QUARTER : BANK + (part + 1) * QUARTER])
+            nc.vector.tensor_tensor(out=in_order(gained[LAST][:, BANK:])[:, :, rows], in0=sums_view, in1=gains, op=ALU.mult)
+            slope_from_sums(in_order(slopes[LAST][:, BANK:])[:, :, rows], sums_view)
+
+        def last_layer2(c):
+            for part, tag in enumerate(("sums1", "sums0")):
+                if c == 0:
+                    last_out[part] = psum_bank([P, QUARTER], "last_out", tag)
+                cols = slice(part * QUARTER, (part + 1) * QUARTER)
+                mx_pass(last_out[part], a_q[LAST, c], c, w2_sb, w2_sc, cols, c == 0, c == A_PASSES - 1)
+
+        def last_store(part, engine_copy):
+            tile = work.tile([P, QUARTER], F32, name="last_out_sb")
+            engine_copy(out=tile[:], in_=last_out[part][:])
+            nc.sync.dma_start(out=out_rows[:, LAST, part * QUARTER : (part + 1) * QUARTER], in_=tile[:])
+
+        zeros = keep.tile([P, BANK], BF16, name="zeros")
+        nc.vector.memset(zeros[:].bitcast(I32), 0)
+
+        def warm_up(count):
+            bank = psum_bank([P, BANK], "warm_bank", "sums1")
+            for step in range(count):
+                nc.tensor.matmul(bank[:], lhsT=zeros[:, :P], rhs=zeros[:], start=True, stop=True)
+
+        warm_up(5)
+        widen_v(nc.vector.tensor_copy, 0, 1)
+        widen_u(nc.vector.tensor_copy, 0)
+        widen_v(nc.vector.tensor_copy, 1, 1)
+        widen_u(nc.vector.tensor_copy, 1)
+        widen_v(nc.vector.tensor_copy, 2, 2)
+        turn_v(0, 1)
+        turn_u(0)
+        double_u_by_pass(0)
+        empty_v(0)
+        turn_v(1, 1)
+        turn_u(1)
+        empty_v(1)
+        double_u_by_pass(2)
+        spread_z_scale(0, "sums0")
+        warm_up(2)
+        widen_u(nc.scalar.copy, 2)
+        spread_z_scale(1, "small")
+        park_u()
+        late_loads()
+        outer(0, 0, 2)
+        outer(0, 2, 2)
+        quantize_p(0, 0)
+        quantize_p(0, 2)
+        outer(1)
+        scale_z(0)
+        quantize_p(1)
+        both_halves(0, range(3))
+        turn_v(2, 2)
+        turn_u(2)
+        turn_z(0)
+        empty_v(2)
+        widen_v(nc.scalar.copy, 4, 4)
+        both_halves(0, range(3, P_PASSES))
+        scale_z(1)
+        sort_z(1)
+        empty_z(0)
+        outer(2)
+        scale_z(2)
+        quantize_z(0)
+        both_halves(1, range(2))
+        turn_z(1)
+        turn_v(4, 2)
+        empty_z(1)
+        empty_v(4)
+        quantize_p(2)
+        sort_z(2)
+        both_halves(1, range(2, P_PASSES))
+        scale_z(3)
+        quantize_z(1)
+        scale_z(4)
+        one_half(0, 0, z_part)
+        one_half(0, 1, z_part)
+        turn_z(2)
+        turn_v(6, 2)
+        sign_of_sums(0, 0)
+        sign_of_sums(0, 1)
+        empty_z(2)
+        gain(0, 0)
+        gain(0, 1)
+        one_half(1, 0, z_part)
+        one_half(1, 1, z_part)
+        quantize_z(2)
+        sign_of_sums(1, 0)
+        sign_of_sums(1, 1)
+        gain(1, 0)
+        slope_from_signs(0, 0)
+        slope_from_signs(0, 1)
+        slope_from_signs(1, 0)
+        empty_v(6)
+
+        for k in range(2, LAST):
+            turned, finished = k - LAG, k - LAG - 1
+            outer(k + 1)
+            slope_from_signs(k - 1, 1)
+            gain(k - 1, 1)
+            turn_z(k + 1)
+            if turned >= 0:
+                turn_a(turned)
+            empty_z(k + 1)
+            if turned >= 0:
+                empty_a(turned)
+            one_half(k, 0)
+            if finished >= 0:
+                layer2(finished)
+            quantize_p(k + 1)
+            rectify(k - 2)
+            if k == LAST - 1:
                 rectify(k - 1)
-            if live(k + 1):
-                z_q[k + 1] = quantize(z_t[k + 1], "z")
-            if live(k - 2):
-                a_q[k - 2] = quantize(a_t[k - 2], "a")
-            if live(k + 1):
-                p_q[k + 1] = quantize(p_t[k + 1], "p")
-            if live(k + 2):
-                scale_z(k + 2)
-            if k == 0:
-                for j in range(PP + ZP):
-                    for half in range(2):
-                        layer1_pass(k, half, j)
-            elif live(k):
-                for j in range(PP + ZP):
-                    layer1_pass(k, 0, j)
-            if live(k):
-                sign_s(k, 0)
-                slope(k, 0)
-                gain(k, 0)
-            if live(k) and k > 0:
-                for j in range(PP + ZP):
-                    layer1_pass(k, 1, j)
-            if live(k - 2):
-                layer2(k - 2)
-            if live(k):
-                sign_s(k, 1)
+            if k + 3 <= LAST:
+                scale_z(k + 3)
+            quantize_z(k + 1)
+            if turned >= 0:
+                quantize_a(turned)
+            sign_of_sums(k, 0)
+            slope_from_signs(k, 0)
+            gain(k, 0)
+            if finished >= 0:
+                store(finished)
+            one_half(k, 1)
+            sign_of_sums(k, 1)
+
+        slope_from_signs(LAST - 1, 1)
+        gain(LAST - 1, 1)
+        turn_a(LAST - 3)
+        turn_a(LAST - 2)
+        empty_a(LAST - 3)
+        empty_a(LAST - 2)
+        layer2(LAST - 4)
+        one_half(LAST, 0)
+        rectify(LAST - 1)
+        quantize_a(LAST - 3)
+        quantize_a(LAST - 2)
+        store(LAST - 4)
+        gain(LAST, 0)
+        slopes[LAST] = work.tile([P, H], BF16, name="slopes")
+        slope_from_sums(in_order(slopes[LAST][:, :BANK]), by_word(sums[LAST, 0][:]))
+        layer2(LAST - 3)
+        last_layer1(0, "sums1")
+        store(LAST - 3)
+        rectify(LAST, 0, 1)
+        last_gain_and_slope(0)
+        last_layer1(1, "sums0")
+
+        turn_a(LAST - 1)
+        turn_a(LAST, 0, 1)
+        layer2(LAST - 2)
+        last_gain_and_slope(1)
+        empty_a(LAST - 1)
+        empty_a(LAST, 0)
+        rectify(LAST, 1, 1)
+        quantize_a(LAST - 1)
+        turn_a(LAST, 1, 1, "sums1")
+        quantize_a(LAST, 0)
+        empty_a(LAST, 1)
+        store(LAST - 2, nc.vector.tensor_copy)
+        layer2(LAST - 1)
+        last_layer2(0)
+        quantize_a(LAST, 1)
+        store(LAST - 1)
+        last_layer2(1)
+        last_store(0, nc.vector.tensor_copy)
+        last_store(1, nc.scalar.copy)

from contextlib import ExitStack

import concourse.mybir as mybir
from concourse.masks import make_identity

B, I, J, Z, H, O = 1024, 64, 32, 1024, 1024, 512
Q = I * J
FLOPS = 2 * B * (Z + Q) * H + 2 * B * H * O

F32 = mybir.dt.float32
BF16 = mybir.dt.bfloat16
I32 = mybir.dt.int32
U32 = mybir.dt.uint32
U8 = mybir.dt.uint8
FP8 = mybir.dt.float8_e4m3fn
FP8X4 = mybir.dt.float8_e4m3fn_x4
ALU = mybir.AluOpType
ACT = mybir.ActivationFunctionType

P = 128
TILES = B // P
LAST = TILES - 1
BANK = 512
K_PASS = 512
Z_PASSES, P_PASSES, A_PASSES = Z // K_PASS, Q // K_PASS, H // K_PASS
BLOCKS = 16
BLOCK_ROWS = 8
QUARTER = BANK // 2
NEAR = 3
LAG = 3
SMALL_BANKS = 4


def tile_outerproductpnntwolayer_w8_kernel(
    tc, z_bytes, z_scale, u, v, wz_words, wz_scales, wp_words, wp_scales, g, w2_words, w2_scales, out
):
    nc = tc.nc
    with ExitStack() as ctx:
        keep = ctx.enter_context(tc.tile_pool(name="keep", bufs=1))
        work = ctx.enter_context(tc.tile_pool(name="work", bufs=3))
        psum = ctx.enter_context(tc.psum_pool(name="psum", bufs=1))
        ctx.enter_context(tc.manual_schedule())

        def psum_bank(shape, name, tag="small"):
            return psum.tile(shape, F32, name=name, tag=tag, bufs=SMALL_BANKS if tag == "small" else 2)

        ident = keep.tile([P, P], F32, name="ident")
        make_identity(nc, ident[:])

        wp_sc = keep.tile([P, H], U8, name="wp_sc", align_bytes=64)
        wz_sc = keep.tile([P, H], U8, name="wz_sc", align_bytes=64)
        w2_sc = keep.tile([P, O], U8, name="w2_sc", align_bytes=64)
        for scale_tile in (wp_sc, wz_sc, w2_sc):
            nc.vector.memset(scale_tile[:].bitcast(I32), 0)

        def load_scales(queue, scale_tile, scales):
            passes = scales.shape[0]
            for quad in range(4):
                queue.dma_start(
                    out=scale_tile[32 * quad : 32 * quad + 4 * passes, :].bitcast(I32),
                    in_=scales[:, 4 * quad : 4 * quad + 4, :].bitcast(I32),
                )

        def load_codes(codes, c, name):
            tile = keep.tile([P, codes.shape[2]], U32, name=name, align_bytes=64)
            nc.sync.dma_start(out=tile[:].bitcast(I32), in_=codes[c].rearrange("p n t -> p (n t)").bitcast(I32))
            return tile

        z_rows = z_bytes.rearrange("(b n) k -> b n k", n=TILES)
        out_rows = out.rearrange("(b n) o -> b n o", n=TILES)
        z_raw = {}

        def load_z(pair):
            tile = keep.tile([P, 2, Z], U8, name="z_raw%d" % pair, align_bytes=64)
            nc.sync.dma_start(out=tile[:], in_=z_rows[:, 2 * pair : 2 * pair + 2, :])
            z_raw[pair] = tile

        u_sb = keep.tile([P, TILES * I], BF16, name="u_sb")
        nc.sync.dma_start(out=u_sb[:], in_=u.rearrange("(b n) i -> b (n i)", n=TILES))
        v_sb = keep.tile([P, TILES * J], BF16, name="v_sb")
        nc.sync.dma_start(out=v_sb[:], in_=v.rearrange("(b n) j -> b (n j)", n=TILES))
        zs_per_row = Z // P
        zs_rows = keep.tile([P, zs_per_row], F32, name="zs_rows")
        nc.sync.dma_start(out=zs_rows[:], in_=z_scale.rearrange("o (a m) -> a (o m)", a=P))
        load_scales(nc.scalar, wp_sc, wp_scales)
        wp_sb = [load_codes(wp_words, c, "wp_sb%d" % c) for c in range(2)]
        load_z(0)
        wp_sb.extend(load_codes(wp_words, c, "wp_sb%d" % c) for c in range(2, P_PASSES))

        v_words = v_sb[:].bitcast(F32).rearrange("b (n r w) -> b n w r", n=TILES, w=2)
        u_doubled, u_wide, v_wide, u_by_pass = {}, {}, {}, {}
        u_bank, u_far, v_bank, v_t = {}, {}, {}, {}

        def double_u(first, count):
            tile = keep.tile([P, count * I, 2], BF16, name="u_doubled%d" % first)
            nc.scalar.activation(
                out=tile[:],
                in_=u_sb[:, first * I : (first + count) * I].unsqueeze(2).to_broadcast([P, count * I, 2]),
                func=ACT.Identity,
            )
            words = tile[:].rearrange("b i e -> b (i e)").bitcast(F32)
            for n in range(count):
                u_doubled[first + n] = words[:, n * I : (n + 1) * I]

        def widen_u(engine_copy, n):
            tile = work.tile([P, I, BLOCK_ROWS], F32, name="u_wide", bufs=TILES)
            engine_copy(out=tile[:], in_=u_doubled[n].unsqueeze(2).to_broadcast([P, I, BLOCK_ROWS]))
            u_wide[n] = tile[:].rearrange("b i r -> b (i r)")

        def turn_u(n):
            bank = psum_bank([P, P_PASSES, P], "u_bank")
            for c in range(P_PASSES):
                nc.tensor.transpose(bank[:, c, :], u_wide[n][:, c * P : (c + 1) * P], ident[:])
            u_bank[n] = bank

        def double_u_by_pass(first):
            shape = [P, 2, TILES, BLOCKS, 2]
            tile = keep.tile(shape, BF16, name="u_by_pass%d" % first)
            columns = u_sb[:].rearrange("b (n c q) -> b c n q", n=TILES, c=P_PASSES)[:, first : first + 2]
            nc.scalar.copy(out=tile[:], in_=columns.unsqueeze(4).to_broadcast(shape))
            words = tile[:].rearrange("b c n q e -> b (c n q e)").bitcast(F32)
            for j in range(2):
                u_by_pass[first + j] = words[:, j * P : (j + 1) * P]

        parked = out_rows[:, LAST, :]

        def park_u():
            bank = psum_bank([P, P_PASSES, P], "park_bank")
            for c in range(P_PASSES):
                nc.tensor.transpose(bank[:, c, :], u_by_pass[c], ident[:])
            rows = keep.tile([P, BANK], F32, name="u_rows")
            nc.scalar.copy(out=rows[:], in_=bank[:].rearrange("p c b -> p (c b)"))
            nc.sync.dma_start(out=parked[BLOCKS * NEAR :, :], in_=rows[BLOCKS * NEAR :, :])

        def fetch_u(n):
            tile = keep.tile([P, BANK], F32, name="u_far%d" % n)
            rows = parked[BLOCKS * n : BLOCKS * (n + 1), :]
            nc.sync.dma_start(out=tile[:], in_=rows.unsqueeze(1).to_broadcast([BLOCKS, BLOCK_ROWS, BANK]))
            u_far[n] = tile

        def widen_v(engine_copy, first, count):
            shape = [P, count, 2, BLOCKS, BLOCK_ROWS]
            tile = keep.tile(shape, F32, name="v_wide%d" % first)
            engine_copy(out=tile[:], in_=v_words[:, first : first + count].unsqueeze(3).to_broadcast(shape))
            for j in range(count):
                v_wide[first + j] = tile[:, j].rearrange("b w q r -> b w (q r)")

        def turn_v(first, count):
            bank = psum_bank([P, count, 2, P], "v_bank")
            for j in range(count):
                for w in range(2):
                    nc.tensor.transpose(bank[:, j, w, :], v_wide[first + j][:, w, :], ident[:])
            v_bank[first] = bank

        def empty_v(first):
            count = v_bank[first].shape[1]
            tile = keep.tile([P, count, P, 2], F32, name="v_t%d" % first)
            nc.scalar.copy(out=tile[:], in_=v_bank[first][:].rearrange("p n w b -> p n b w"))
            for j in range(count):
                v_t[first + j] = tile[:, j].rearrange("p b w -> p (b w)").bitcast(BF16)

        double_u(0, 1)
        double_u(1, NEAR - 1)
        load_z(1)
        load_scales(nc.sync, wz_sc, wz_scales)
        wz_sb = [load_codes(wz_words, c, "wz_sb%d" % c) for c in range(Z_PASSES)]
        load_z(2)
        g_sb = keep.tile([P, H], BF16, name="g_sb")
        w2_sb = []

        def late_loads():
            nc.sync.dma_start(out=g_sb[:], in_=g.partition_broadcast(P))
            fetch_u(NEAR)
            load_z(3)
            for n in range(NEAR + 1, TILES):
                fetch_u(n)
            load_scales(nc.sync, w2_sc, w2_scales)
            w2_sb.extend(load_codes(w2_words, c, "w2_sb%d" % c) for c in range(A_PASSES))

        zs_sb = keep.tile([P, Z], F32, name="zs_sb")
        z_bf, z_sorted, z_bank, z_t = {}, {}, {}, {}

        def spread_z_scale(half, tag):
            count = zs_per_row // 2
            columns = zs_sb[:].rearrange("b (a m) -> b a m", m=zs_per_row)
            bank = psum_bank([P, count, P], "zs_bank", tag)
            for j in range(count):
                m = count * half + j
                nc.tensor.transpose(bank[:, j, :], zs_rows[:, m : m + 1].to_broadcast([P, P]), ident[:])
            nc.scalar.copy(out=columns[:, :, count * half : count * (half + 1)], in_=bank[:].rearrange("b j a -> b a j"))

        def scale_z(n):
            tile = work.tile([P, Z], BF16, name="z_bf", align_bytes=64, bufs=5)
            nc.vector.tensor_tensor(out=tile[:], in0=z_raw[n // 2][:, n % 2, :].bitcast(FP8), in1=zs_sb[:], op=ALU.mult)
            z_bf[n] = tile

        def sort_z(n):
            tile = work.tile([P, Z_PASSES, 2, P], F32, name="z_sorted")
            nc.scalar.copy(out=tile[:], in_=z_bf[n][:].bitcast(F32).rearrange("b (c p w) -> b c w p", c=Z_PASSES, w=2))
            z_sorted[n] = tile

        def turn_z(n):
            bank = psum_bank([P, Z_PASSES, 2, P], "z_bank")
            words = z_bf[n][:].bitcast(F32)
            for c in range(Z_PASSES):
                for w in range(2):
                    if n in z_sorted:
                        source = z_sorted[n][:, c, w, :]
                    else:
                        source = words[:, 2 * P * c + w : 2 * P * (c + 1) : 2]
                    nc.tensor.transpose(bank[:, c, w, :], source, ident[:])
            z_bank[n] = bank

        def empty_words(bank, name):
            count = bank.shape[1]
            tile = work.tile([P, count * K_PASS], BF16, name=name, align_bytes=64)
            nc.scalar.copy(
                out=tile[:].bitcast(F32).rearrange("p (c b w) -> p c b w", c=count, w=2),
                in_=bank[:].rearrange("p c w b -> p c b w"),
            )
            return tile

        def empty_z(n):
            z_t[n] = empty_words(z_bank[n], "z_t")

        p_t = {}

        def outer(n, first=0, count=P_PASSES):
            tile = work.tile([P, count * K_PASS], BF16, name="p_t", align_bytes=64, bufs=4)
            shape = [P, count, P, 2, 2]
            u_words = u_far[n][:] if n >= NEAR else u_bank[n][:].rearrange("p c b -> p (c b)")
            u_twice = u_words.bitcast(BF16).rearrange("p (c b e) -> p c b e", c=P_PASSES, e=2)
            nc.vector.tensor_tensor(
                out=tile[:].rearrange("p (c b w e) -> p c b w e", c=count, w=2, e=2),
                in0=u_twice[:, first : first + count].unsqueeze(3).to_broadcast(shape),
                in1=v_t[n].rearrange("p (b w e) -> p b w e", w=2, e=2).unsqueeze(1).to_broadcast(shape),
                op=ALU.mult,
            )
            p_t[n, first] = tile

        z_q, p_q, a_q = {}, {}, {}
        a_t = {}

        def quantize(source, name, into, n, first):
            width = source.shape[1] // 4
            codes = work.tile([P, width], U32, name=name + "_codes", align_bytes=64, bufs=4)
            scales = work.tile([P, width], U8, name=name + "_scales", align_bytes=64, bufs=4)
            nc.vector.quantize_mx(out=codes[:].bitcast(FP8X4), scales=scales[:], in_=source[:])
            for c in range(width // P):
                into[n, first + c] = (codes[:, c * P : (c + 1) * P], scales[:, c * P : (c + 1) * P])

        def quantize_p(n, first=0):
            quantize(p_t[n, first], "p", p_q, n, first)

        def quantize_z(n):
            quantize(z_t[n], "z", z_q, n, 0)

        def quantize_a(n, first=0):
            quantize(a_t[n, first], "a", a_q, n, first)

        def mx_pass(bank, tokens, c, weight, weight_scales, cols, start, stop):
            codes, scales = tokens
            nc.tensor.matmul_mx(
                out=bank[:],
                lhsT=codes.bitcast(FP8X4),
                lhsT_scale=scales,
                rhs=weight[c][:, cols].bitcast(FP8X4),
                rhs_scale=weight_scales[4 * c :, cols],
                start=start,
                stop=stop,
            )

        sums = {}
        layer1_passes = range(P_PASSES + Z_PASSES)
        z_part = layer1_passes[P_PASSES:]

        def layer1_pass(bank, n, cols, j):
            if j < P_PASSES:
                mx_pass(bank, p_q[n, j], j, wp_sb, wp_sc, cols, j == 0, False)
            else:
                mx_pass(bank, z_q[n, j - P_PASSES], j - P_PASSES, wz_sb, wz_sc, cols, False, j == layer1_passes[-1])

        def one_half(n, half, passes=layer1_passes):
            for j in passes:
                if j == 0:
                    sums[n, half] = psum_bank([P, BANK], "sums", "sums%d" % half)
                layer1_pass(sums[n, half], n, slice(half * BANK, (half + 1) * BANK), j)

        def both_halves(n, passes):
            for j in passes:
                for half in range(2):
                    one_half(n, half, [j])

        signs, slopes, gained, a_bf, a_bank = {}, {}, {}, {}, {}

        def by_word(natural):
            return natural.rearrange("b (p w e) -> b w p e", w=2, e=2)

        def in_order(sorted_cols):
            return sorted_cols.rearrange("b (w p e) -> b w p e", w=2, e=2)

        def sign_of_sums(n, half):
            tile = work.tile([P, BANK], BF16, name="signs", bufs=4)
            nc.scalar.activation(out=in_order(tile[:]), in_=by_word(sums[n, half][:]), func=ACT.Sign)
            signs[n, half] = tile

        def slope_from_signs(n, half):
            if half == 0:
                slopes[n] = work.tile([P, H], BF16, name="slopes")
            nc.scalar.activation(
                out=slopes[n][:, half * BANK : (half + 1) * BANK],
                in_=signs[n, half][:],
                func=ACT.Identity,
                scale=0.375,
                bias=0.625,
            )

        def slope_from_sums(slope_view, sums_view):
            nc.vector.tensor_scalar(out=slope_view, in0=sums_view, scalar1=0.0, scalar2=0.25, op0=ALU.is_ge, op1=ALU.max)

        def gain(n, half):
            cols = slice(half * BANK, (half + 1) * BANK)
            if half == 0:
                gained[n] = work.tile([P, H], BF16, name="gained")
            nc.vector.tensor_tensor(
                out=in_order(gained[n][:, cols]), in0=by_word(sums[n, half][:]), in1=by_word(g_sb[:, cols]), op=ALU.mult
            )

        def rectify(n, first=0, count=A_PASSES):
            cols = slice(first * K_PASS, (first + count) * K_PASS)
            tile = work.tile([P, count * K_PASS], BF16, name="a_bf", bufs=6)
            nc.vector.tensor_tensor(out=tile[:], in0=gained[n][:, cols], in1=slopes[n][:, cols], op=ALU.mult)
            a_bf[n, first] = tile

        def turn_a(n, first=0, count=A_PASSES, tag="small"):
            bank = psum_bank([P, count, 2, P], "a_bank", tag)
            words = a_bf[n, first][:].bitcast(F32)
            for c in range(count):
                for w in range(2):
                    nc.tensor.transpose(bank[:, c, w, :], words[:, P * (2 * c + w) : P * (2 * c + w + 1)], ident[:])
            a_bank[n, first] = bank

        def empty_a(n, first=0):
            a_t[n, first] = empty_words(a_bank[n, first], "a_t")

        o_bank = {}

        def layer2(n):
            o_bank[n] = psum_bank([P, O], "o_bank")
            for c in range(A_PASSES):
                mx_pass(o_bank[n], a_q[n, c], c, w2_sb, w2_sc, slice(0, O), c == 0, c == A_PASSES - 1)

        def store(n, engine_copy=nc.scalar.copy):
            tile = work.tile([P, O], F32, name="o_sb", bufs=4)
            engine_copy(out=tile[:], in_=o_bank[n][:])
            nc.sync.dma_start(out=out_rows[:, n, :], in_=tile[:])

        last_sums, last_out = {}, {}

        def last_layer1(part, tag):
            last_sums[part] = psum_bank([P, QUARTER], "last_sums", tag)
            for j in layer1_passes:
                layer1_pass(last_sums[part], LAST, slice(BANK + part * QUARTER, BANK + (part + 1) * QUARTER), j)

        def last_gain_and_slope(part):
            rows = slice(part * P // 2, (part + 1) * P // 2)
            sums_view = by_word(last_sums[part][:])
            gains = by_word(g_sb[:, BANK + part * QUARTER : BANK + (part + 1) * QUARTER])
            nc.vector.tensor_tensor(out=in_order(gained[LAST][:, BANK:])[:, :, rows], in0=sums_view, in1=gains, op=ALU.mult)
            slope_from_sums(in_order(slopes[LAST][:, BANK:])[:, :, rows], sums_view)

        def last_layer2(c):
            for part, tag in enumerate(("sums1", "sums0")):
                if c == 0:
                    last_out[part] = psum_bank([P, QUARTER], "last_out", tag)
                cols = slice(part * QUARTER, (part + 1) * QUARTER)
                mx_pass(last_out[part], a_q[LAST, c], c, w2_sb, w2_sc, cols, c == 0, c == A_PASSES - 1)

        def last_store(part, engine_copy):
            tile = work.tile([P, QUARTER], F32, name="last_out_sb")
            engine_copy(out=tile[:], in_=last_out[part][:])
            nc.sync.dma_start(out=out_rows[:, LAST, part * QUARTER : (part + 1) * QUARTER], in_=tile[:])

        zeros = keep.tile([P, BANK], BF16, name="zeros")
        nc.vector.memset(zeros[:].bitcast(I32), 0)

        def warm_up(count):
            bank = psum_bank([P, BANK], "warm_bank", "sums1")
            for step in range(count):
                nc.tensor.matmul(bank[:], lhsT=zeros[:, :P], rhs=zeros[:], start=True, stop=True)

        warm_up(5)
        widen_v(nc.vector.tensor_copy, 0, 1)
        widen_u(nc.vector.tensor_copy, 0)
        widen_v(nc.vector.tensor_copy, 1, 1)
        widen_u(nc.vector.tensor_copy, 1)
        widen_v(nc.vector.tensor_copy, 2, 2)
        turn_v(0, 1)
        turn_u(0)
        double_u_by_pass(0)
        empty_v(0)
        turn_v(1, 1)
        turn_u(1)
        empty_v(1)
        double_u_by_pass(2)
        spread_z_scale(0, "sums0")
        warm_up(2)
        widen_u(nc.scalar.copy, 2)
        spread_z_scale(1, "small")
        park_u()
        late_loads()
        outer(0, 0, 2)
        outer(0, 2, 2)
        quantize_p(0, 0)
        quantize_p(0, 2)
        outer(1)
        scale_z(0)
        quantize_p(1)
        both_halves(0, range(3))
        turn_v(2, 2)
        turn_u(2)
        turn_z(0)
        empty_v(2)
        widen_v(nc.scalar.copy, 4, 4)
        both_halves(0, range(3, P_PASSES))
        scale_z(1)
        sort_z(1)
        empty_z(0)
        outer(2)
        scale_z(2)
        quantize_z(0)
        both_halves(1, range(2))
        turn_z(1)
        turn_v(4, 2)
        empty_z(1)
        empty_v(4)
        quantize_p(2)
        sort_z(2)
        both_halves(1, range(2, P_PASSES))
        scale_z(3)
        quantize_z(1)
        scale_z(4)
        one_half(0, 0, z_part)
        one_half(0, 1, z_part)
        turn_z(2)
        turn_v(6, 2)
        sign_of_sums(0, 0)
        sign_of_sums(0, 1)
        empty_z(2)
        gain(0, 0)
        gain(0, 1)
        one_half(1, 0, z_part)
        one_half(1, 1, z_part)
        quantize_z(2)
        sign_of_sums(1, 0)
        sign_of_sums(1, 1)
        gain(1, 0)
        slope_from_signs(0, 0)
        slope_from_signs(0, 1)
        slope_from_signs(1, 0)
        empty_v(6)

        for k in range(2, LAST):
            turned, finished = k - LAG, k - LAG - 1
            outer(k + 1)
            slope_from_signs(k - 1, 1)
            gain(k - 1, 1)
            turn_z(k + 1)
            if turned >= 0:
                turn_a(turned)
            empty_z(k + 1)
            if turned >= 0:
                empty_a(turned)
            one_half(k, 0)
            if finished >= 0:
                layer2(finished)
            quantize_p(k + 1)
            rectify(k - 2)
            if k == LAST - 1:
                rectify(k - 1)
            if k + 3 <= LAST:
                scale_z(k + 3)
            quantize_z(k + 1)
            if turned >= 0:
                quantize_a(turned)
            sign_of_sums(k, 0)
            slope_from_signs(k, 0)
            gain(k, 0)
            if finished >= 0:
                store(finished)
            one_half(k, 1)
            sign_of_sums(k, 1)

        slope_from_signs(LAST - 1, 1)
        gain(LAST - 1, 1)
        turn_a(LAST - 3)
        turn_a(LAST - 2)
        empty_a(LAST - 3)
        empty_a(LAST - 2)
        layer2(LAST - 4)
        one_half(LAST, 0)
        rectify(LAST - 1)
        quantize_a(LAST - 3)
        quantize_a(LAST - 2)
        store(LAST - 4)
        gain(LAST, 0)
        slopes[LAST] = work.tile([P, H], BF16, name="slopes")
        slope_from_sums(in_order(slopes[LAST][:, :BANK]), by_word(sums[LAST, 0][:]))
        layer2(LAST - 3)
        last_layer1(0, "sums1")
        store(LAST - 3)
        rectify(LAST, 0, 1)
        last_gain_and_slope(0)
        last_layer1(1, "sums0")

        turn_a(LAST - 1)
        turn_a(LAST, 0, 1)
        layer2(LAST - 2)
        last_gain_and_slope(1)
        empty_a(LAST - 1)
        empty_a(LAST, 0)
        rectify(LAST, 1, 1)
        quantize_a(LAST - 1)
        turn_a(LAST, 1, 1, "sums1")
        quantize_a(LAST, 0)
        empty_a(LAST, 1)
        store(LAST - 2, nc.vector.tensor_copy)
        layer2(LAST - 1)
        last_layer2(0)
        quantize_a(LAST, 1)
        store(LAST - 1)
        last_layer2(1)
        last_store(0, nc.vector.tensor_copy)
        last_store(1, nc.scalar.copy)
